import numpy as np
import ml_dtypes


def mxq(x, axis, fmt="e4m3"):
    dtype, down = {"e4m3": (ml_dtypes.float8_e4m3fn, 7), "e5m2": (ml_dtypes.float8_e5m2, 14)}[fmt]
    v = np.moveaxis(np.asarray(x, np.float32).astype(ml_dtypes.bfloat16).astype(np.float64), axis, -1)
    blocks = v.reshape(v.shape[:-1] + (-1, 32))
    amax = np.abs(blocks).max(-1, keepdims=True)
    byte = np.maximum(np.where(amax > 0, np.frexp(amax)[1] - 1 + 127, 0) - down, 1)
    scale = np.exp2(byte - 127.0)
    codes = (blocks / scale).astype(np.float32).astype(dtype).astype(np.float64)
    return np.moveaxis((codes * scale).reshape(v.shape), -1, axis)


WIDE = False


def mx_kscale(k):
    if not WIDE:
        return np.ones(k)
    levels = np.array([30, -30])
    if k % 512:
        return np.exp2(np.random.permutation(np.resize(levels, k // 32))).repeat(32)
    a = np.empty((k // 512, 16))
    for p in range(k // 512):
        a[p, :8] = np.random.permutation(np.resize(levels, 8))
        for g in range(8):
            far = levels[np.abs(levels - a[p, g]) >= 10]
            a[p, g + 8] = far[np.random.randint(len(far))]
    return np.exp2(a.ravel()).repeat(32)


def f64(x):
    return np.asarray(x).astype(np.float64)


def striped(idx):
    return np.tile(np.asarray(idx).reshape(-1, 16).T, (8, 1)).astype(np.uint16)


def unstriped(offs):
    return offs[:16].T.reshape(-1).astype(np.int64)


E2M1 = np.array([0.0, 0.5, 1.0, 1.5, 2.0, 3.0, 4.0, 6.0, -0.0, -0.5, -1.0, -1.5, -2.0, -3.0, -4.0, -6.0])


def pack_weight(w, fmt):
    k, n = w.shape
    w = f64(np.asarray(w, np.float32).astype(ml_dtypes.bfloat16)).reshape(k // 32, 32, n)
    amax = np.abs(w).max(1)
    if fmt in ("e4m3", "e5m2"):
        byte = np.frexp(amax)[1] - 1 + 127 - (7 if fmt == "e4m3" else 14)
    else:
        mant, ex = np.frexp(amax / 6.0)
        byte = np.where(mant > 0.5, ex, ex - 1) + 127
    byte = np.clip(np.where(amax > 0, byte, 1), 1, 254)
    scaled = (w * np.exp2(127.0 - byte)[:, None, :]).reshape(k, n).astype(np.float32)
    by_word = np.ascontiguousarray(scaled.reshape(k // 512, 128, 4, n).transpose(0, 1, 3, 2))
    if fmt in ("e4m3", "e5m2"):
        words = by_word.astype(ml_dtypes.float8_e4m3fn if fmt == "e4m3" else ml_dtypes.float8_e5m2).view(np.uint8)
    else:
        c = by_word.astype(ml_dtypes.float4_e2m1fn).view(np.uint8) & 0xF
        words = (c[..., 0::2] | (c[..., 1::2] << 4)).reshape(k // 512, 128, 2 * n)
    return np.ascontiguousarray(words), np.ascontiguousarray(byte.astype(np.uint8).reshape(k // 512, 16, n))


def unpack_weight(words, scales, fmt):
    g, _, n = scales.shape
    words = np.ascontiguousarray(words).reshape(g, 128, n, -1)
    if fmt in ("e4m3", "e5m2"):
        vals = words.view(ml_dtypes.float8_e4m3fn if fmt == "e4m3" else ml_dtypes.float8_e5m2).astype(np.float64)
    else:
        nib = np.empty((g, 128, n, 4), np.uint8)
        nib[..., 0::2] = words & 0xF
        nib[..., 1::2] = words >> 4
        vals = E2M1[nib]
    vals = vals * np.repeat(np.exp2(scales.astype(np.float64) - 127.0), 8, axis=1)[..., None]
    return vals.transpose(0, 1, 3, 2).reshape(g * 512, n)


def e4m3fn_bytes(y):
    return np.clip(np.asarray(y, np.float64), -448.0, 448.0).astype(np.float32).astype(ml_dtypes.float8_e4m3fn).view(np.uint8)


def e4m3fn_values(b):
    return np.asarray(b, np.uint8).view(ml_dtypes.float8_e4m3fn).astype(np.float64)


K, T, J, R, V, D, N = 512, 1024, 256, 512, 1024, 2048, 256


def setup_inputs():
    n = np.random.standard_normal
    idx = np.random.permutation(V)[:R]
    idx2 = np.random.permutation(T)[:J]
    idx3 = np.random.permutation(D)[:J]
    fk = mx_kscale(K)
    fr = mx_kscale(R)
    xtp = pack_weight(n((K, T)) / fk[:, None], "e5m2")
    wtp = pack_weight(n((K, V)) * 1 / np.sqrt(K) * fk[:, None], "e2m1")
    wbp = pack_weight(n((R, N)) * 1 / np.sqrt(R) / fr[:, None], "e2m1")
    return {
        "xt_words": xtp[0],
        "xt_scales": xtp[1],
        "wt_words": wtp[0],
        "wt_scales": wtp[1],
        "ca": e4m3fn_bytes(60.0 * n((R, D))),
        "st": (np.random.uniform(0.004, 0.012, (R, 1)) * fr[:, None]).astype(np.float32),
        "wb_words": wbp[0],
        "wb_scales": wbp[1],
        "offs": striped(idx),
        "offs2": striped(idx2),
        "offs3": striped(idx3),
    }


def reference(xt_words, xt_scales, wt_words, wt_scales, ca, st, wb_words, wb_scales, offs, offs2, offs3):
    idx = unstriped(offs)
    idx2 = unstriped(offs2)
    idx3 = unstriped(offs3)
    xtu = unpack_weight(xt_words, xt_scales, "e5m2")
    wtu = unpack_weight(wt_words, wt_scales, "e2m1")
    wbu = unpack_weight(wb_words, wb_scales, "e2m1")
    wtidxg = wtu[:, idx]
    xtidx2g = xtu[:, idx2]
    a = wtidxg.T @ xtidx2g
    g1 = e4m3fn_values(ca)[:, idx3] * f64(st)
    g2 = np.pad(g1, ((0, 0), (1, 0)))[:, :J]
    hid = a * (g1 - g2)
    hidq = mxq(hid, 0, "e4m3")
    p = wbu.T @ hidq
    return p

@@ -1,0 +1,139 @@
+from contextlib import ExitStack
+
+import concourse.mybir as mybir
+
+K, T, J, R, V, D, N = 512, 1024, 256, 512, 1024, 2048, 256
+FLOPS = 2 * K * R * J + 2 * R * N * J
+
+F32 = mybir.dt.float32
+BF16 = mybir.dt.bfloat16
+I32 = mybir.dt.int32
+U32 = mybir.dt.uint32
+U16 = mybir.dt.uint16
+U8 = mybir.dt.uint8
+E4M3 = mybir.dt.float8_e4m3fn
+E4M3X4 = mybir.dt.float8_e4m3fn_x4
+E5M2X4 = mybir.dt.float8_e5m2_x4
+E2M1X4 = mybir.dt.float4_e2m1fn_x4
+ALU = mybir.AluOpType
+ACT = mybir.ActivationFunctionType
+
+P = 128
+PACK = 4
+HALF = J // 2
+LIST_COLS = HALF // 16
+G_COLS = J + 8
+
+
+def load_scale_rows(queue, plane, scales):
+    for q in range(4):
+        queue.dma_start(plane[32 * q : 32 * q + 4, :].bitcast(I32), scales[0, 4 * q : 4 * q + 4, :].bitcast(I32))
+
+
+def tile_list_increments_kernel(tc, xt_words, xt_scales, wt_words, wt_scales, ca, st, wb_words, wb_scales, offs, offs2, offs3, out):
+    nc = tc.nc
+    with ExitStack() as ctx:
+        sb = ctx.enter_context(tc.tile_pool(name="sb", bufs=1))
+        ps = ctx.enter_context(tc.psum_pool(name="ps", bufs=1))
+
+        wt_list = sb.tile([P, R // 16], U16, name="wt_list")
+        xt_list = sb.tile([P, J // 16], U16, name="xt_list")
+        ca_list = sb.tile([P, J // 16], U16, name="ca_list")
+        wt_w = sb.tile([P, V], U16, name="wt_w", align_bytes=64)
+        wt_s = sb.tile([P, V], U8, name="wt_s", align_bytes=64)
+        xt_w = sb.tile([P, T], U32, name="xt_w", align_bytes=64)
+        xt_s = sb.tile([P, T], U8, name="xt_s", align_bytes=64)
+        wb_w = sb.tile([P, 2 * N], U8, name="wb_w", align_bytes=64)
+        wb_s = sb.tile([P, N], U8, name="wb_s", align_bytes=64)
+        ca_t = [sb.tile([P, D], U8, name="ca_t%d" % t, align_bytes=64) for t in range(PACK)]
+        step = sb.tile([P, PACK], F32, name="step")
+        g = [sb.tile([P, G_COLS], F32, name="g%d" % t, align_bytes=64) for t in range(PACK)]
+
+        nc.vector.memset(wt_s[:].bitcast(I32), 0)
+        nc.vector.memset(xt_s[:].bitcast(I32), 0)
+        nc.vector.memset(wb_s[:].bitcast(I32), 0)
+        for t in range(PACK):
+            nc.vector.memset(g[t][:, 0:1], 0.0)
+
+        ca_rows = ca.rearrange("(p t) d -> p t d", t=PACK)
+        nc.sync.dma_start(wt_list[:], offs)
+        nc.sync.dma_start(wt_w[:].bitcast(I32), wt_words[0].bitcast(I32))
+        load_scale_rows(nc.scalar, wt_s, wt_scales)
+        nc.sync.dma_start(ca_list[:], offs3)
+        nc.sync.dma_start(ca_t[0][:], ca_rows[:, 0, :])
+        nc.sync.dma_start(step[:], st.rearrange("(p t) o -> p (t o)", t=PACK))
+        for t in range(1, PACK):
+            nc.sync.dma_start(ca_t[t][:], ca_rows[:, t, :])
+        nc.sync.dma_start(xt_list[:], offs2)
+        nc.sync.dma_start(xt_w[:].bitcast(I32), xt_words[0].rearrange("p c r -> p (c r)").bitcast(I32))
+        load_scale_rows(nc.sync, xt_s, xt_scales)
+        nc.sync.dma_start(wb_w[:].bitcast(I32), wb_words[0].bitcast(I32))
+        load_scale_rows(nc.sync, wb_s, wb_scales)
+
+        wt_wg = sb.tile([P, R], U16, name="wt_wg", align_bytes=64)
+        nc.vector.tensor_copy(wt_wg[:], wt_w[:].indirect(wt_list[:]))
+        wt_sg = sb.tile([P, R], U8, name="wt_sg", align_bytes=64)
+        nc.vector.tensor_copy(wt_sg[:].rearrange("p (t m) -> p m t", t=PACK), wt_s[:].indirect(wt_list[:]))
+        wt_wd = sb.tile([P, R], U16, name="wt_wd", align_bytes=64)
+        nc.vector.tensor_copy(wt_wd[:].rearrange("p (t m) -> p t m", t=PACK), wt_wg[:].rearrange("p (m t) -> p t m", t=PACK))
+
+        inc = sb.tile([P, PACK, J], F32, name="inc", align_bytes=64)
+        for t in range(PACK):
+            ca_g = sb.tile([P, J], U8, name="ca_g%d" % t, align_bytes=64)
+            nc.vector.tensor_copy(ca_g[:], ca_t[t][:].indirect(ca_list[:]))
+            nc.scalar.activation(g[t][:, 1 : J + 1], ca_g[:].bitcast(E4M3), ACT.Copy, scale=step[:, t : t + 1])
+            nc.gpsimd.tensor_tensor(inc[:, t, :], g[t][:, 1 : J + 1], g[t][:, 0:J], ALU.subtract)
+
+        a_ps = []
+        for h in range(2):
+            cols = xt_list[:, h * LIST_COLS : (h + 1) * LIST_COLS]
+            xt_wg = sb.tile([P, HALF], U32, name="xt_wg%d" % h, align_bytes=64)
+            nc.vector.tensor_copy(xt_wg[:], xt_w[:].indirect(cols))
+            xt_sg = sb.tile([P, HALF], U8, name="xt_sg%d" % h, align_bytes=64)
+            nc.vector.tensor_copy(xt_sg[:], xt_s[:].indirect(cols))
+            bank = ps.tile([P, PACK, HALF], F32, name="a_ps%d" % h)
+            for t in range(PACK):
+                nc.tensor.matmul_mx(
+                    out=bank[:, t, :],
+                    lhsT=wt_wd[:, t * P : (t + 1) * P].bitcast(E2M1X4),
+                    lhsT_scale=wt_sg[:, t * P : (t + 1) * P],
+                    rhs=xt_wg[:].bitcast(E5M2X4),
+                    rhs_scale=xt_sg[:],
+                    start=True,
+                    stop=True,
+                )
+            a_ps.append(bank)
+
+        hid = []
+        for h in range(2):
+            hid_h = sb.tile([P, HALF * PACK], BF16, name="hid%d" % h, align_bytes=64)
+            nc.vector.tensor_tensor(
+                hid_h[:].rearrange("p (c i t) -> p c t i", i=2, t=PACK),
+                a_ps[h][:].rearrange("p t (c i) -> p c t i", i=2),
+                inc[:, :, h * HALF : (h + 1) * HALF].rearrange("p t (c i) -> p c t i", i=2),
+                ALU.mult,
+            )
+            hid.append(hid_h)
+
+        res = [sb.tile([P, J], F32, name="res%d" % b, align_bytes=64) for b in range(2)]
+        for h in range(2):
+            hid_w = sb.tile([P, HALF], U32, name="hid_w%d" % h, align_bytes=64)
+            hid_s = sb.tile([P, HALF], U8, name="hid_s%d" % h, align_bytes=64)
+            nc.vector.quantize_mx(out=hid_w[:].bitcast(E4M3X4), scales=hid_s[:], in_=hid[h][:])
+            for b in range(2):
+                acc = ps.tile([P, HALF], F32, name="o_ps%d%d" % (h, b))
+                nc.tensor.matmul_mx(
+                    out=acc[:],
+                    lhsT=wb_w[:, 2 * b * P : 2 * (b + 1) * P].bitcast(E2M1X4),
+                    lhsT_scale=wb_s[:, b * P : (b + 1) * P],
+                    rhs=hid_w[:].bitcast(E4M3X4),
+                    rhs_scale=hid_s[:],
+                    start=True,
+                    stop=True,
+                )
+                if b == 0:
+                    nc.scalar.copy(res[b][:, h * HALF : (h + 1) * HALF], acc[:])
+                else:
+                    nc.vector.tensor_copy(res[b][:, h * HALF : (h + 1) * HALF], acc[:])
+        nc.scalar.dma_start(out[0:P, :], res[0][:])
+        nc.sync.dma_start(out[P : 2 * P, :], res[1][:])

@@ -20,14 +20,19 @@ ACT = mybir.ActivationFunctionType
 
 P = 128
 PACK = 4
-HALF = J // 2
-LIST_COLS = HALF // 16
+GROUP = 16
+QUADRANT = 32
+SCALE_ROWS = 4
+HALVES = 2
+HALF = J // HALVES
 G_COLS = J + 8
+PAIR = 2
 
 
-def load_scale_rows(queue, plane, scales):
-    for q in range(4):
-        queue.dma_start(plane[32 * q : 32 * q + 4, :].bitcast(I32), scales[0, 4 * q : 4 * q + 4, :].bitcast(I32))
+def load_scale_rows(nc, plane, scales):
+    for q in range(P // QUADRANT):
+        rows = scales[0, SCALE_ROWS * q : SCALE_ROWS * (q + 1), :]
+        nc.sync.dma_start(plane[QUADRANT * q : QUADRANT * q + SCALE_ROWS, :].bitcast(I32), rows.bitcast(I32))
 
 
 def tile_list_increments_kernel(tc, xt_words, xt_scales, wt_words, wt_scales, ca, st, wb_words, wb_scales, offs, offs2, offs3, out):
@@ -36,61 +41,67 @@ def tile_list_increments_kernel(tc, xt_words, xt_scales, wt_words, wt_scales, ca
         sb = ctx.enter_context(tc.tile_pool(name="sb", bufs=1))
         ps = ctx.enter_context(tc.psum_pool(name="ps", bufs=1))
 
-        wt_list = sb.tile([P, R // 16], U16, name="wt_list")
-        xt_list = sb.tile([P, J // 16], U16, name="xt_list")
-        ca_list = sb.tile([P, J // 16], U16, name="ca_list")
+        wt_list = sb.tile([P, R // GROUP], U16, name="wt_list")
+        xt_list = sb.tile([P, J // GROUP], U16, name="xt_list")
+        ca_list = sb.tile([P, J // GROUP], U16, name="ca_list")
         wt_w = sb.tile([P, V], U16, name="wt_w", align_bytes=64)
         wt_s = sb.tile([P, V], U8, name="wt_s", align_bytes=64)
         xt_w = sb.tile([P, T], U32, name="xt_w", align_bytes=64)
         xt_s = sb.tile([P, T], U8, name="xt_s", align_bytes=64)
         wb_w = sb.tile([P, 2 * N], U8, name="wb_w", align_bytes=64)
         wb_s = sb.tile([P, N], U8, name="wb_s", align_bytes=64)
-        ca_t = [sb.tile([P, D], U8, name="ca_t%d" % t, align_bytes=64) for t in range(PACK)]
+        ca_t = [sb.tile([P, D], U8, name="ca_t%d" % t, tag="ca_t%d" % t, align_bytes=64) for t in range(PACK)]
         step = sb.tile([P, PACK], F32, name="step")
-        g = [sb.tile([P, G_COLS], F32, name="g%d" % t, align_bytes=64) for t in range(PACK)]
+        g = sb.tile([P, PACK, G_COLS], F32, name="g", align_bytes=64)
+        zero = sb.tile([P, PACK], F32, name="zero")
 
         nc.vector.memset(wt_s[:].bitcast(I32), 0)
         nc.vector.memset(xt_s[:].bitcast(I32), 0)
         nc.vector.memset(wb_s[:].bitcast(I32), 0)
-        for t in range(PACK):
-            nc.vector.memset(g[t][:, 0:1], 0.0)
+        nc.vector.memset(zero[:], 0.0)
 
         ca_rows = ca.rearrange("(p t) d -> p t d", t=PACK)
         nc.sync.dma_start(wt_list[:], offs)
-        nc.sync.dma_start(wt_w[:].bitcast(I32), wt_words[0].bitcast(I32))
-        load_scale_rows(nc.scalar, wt_s, wt_scales)
+        nc.scalar.dma_start(wt_w[:].bitcast(I32), wt_words[0].bitcast(I32))
         nc.sync.dma_start(ca_list[:], offs3)
         nc.sync.dma_start(ca_t[0][:], ca_rows[:, 0, :])
-        nc.sync.dma_start(step[:], st.rearrange("(p t) o -> p (t o)", t=PACK))
+        nc.scalar.dma_start(step[:], st.rearrange("(p t) o -> p (t o)", t=PACK))
         for t in range(1, PACK):
             nc.sync.dma_start(ca_t[t][:], ca_rows[:, t, :])
+        load_scale_rows(nc, wt_s, wt_scales)
         nc.sync.dma_start(xt_list[:], offs2)
+        load_scale_rows(nc, xt_s, xt_scales)
         nc.sync.dma_start(xt_w[:].bitcast(I32), xt_words[0].rearrange("p c r -> p (c r)").bitcast(I32))
-        load_scale_rows(nc.sync, xt_s, xt_scales)
         nc.sync.dma_start(wb_w[:].bitcast(I32), wb_words[0].bitcast(I32))
-        load_scale_rows(nc.sync, wb_s, wb_scales)
+        load_scale_rows(nc, wb_s, wb_scales)
+
+        nc.scalar.activation(g[:, :, 0], zero[:], ACT.Copy)
+
+        inc = sb.tile([P, PACK, J], F32, name="inc", align_bytes=64)
+
+        def increments(t):
+            ca_g = sb.tile([P, J], U8, name="ca_g%d" % t, align_bytes=64)
+            nc.vector.tensor_copy(ca_g[:], ca_t[t][:].indirect(ca_list[:]))
+            nc.scalar.activation(g[:, t, 1 : J + 1], ca_g[:].bitcast(E4M3), ACT.Copy, scale=step[:, t : t + 1])
+            nc.gpsimd.tensor_tensor(inc[:, t, :], g[:, t, 1 : J + 1], g[:, t, 0:J], ALU.subtract)
 
         wt_wg = sb.tile([P, R], U16, name="wt_wg", align_bytes=64)
         nc.vector.tensor_copy(wt_wg[:], wt_w[:].indirect(wt_list[:]))
+        increments(0)
+        wt_wd = sb.tile([P, R], U16, name="wt_wd", tag="ca_t0", align_bytes=64)
+        nc.vector.tensor_copy(wt_wd[:].rearrange("p (t m) -> p t m", t=PACK), wt_wg[:].rearrange("p (m t) -> p t m", t=PACK))
+        for t in range(1, PACK):
+            increments(t)
+
         wt_sg = sb.tile([P, R], U8, name="wt_sg", align_bytes=64)
         nc.vector.tensor_copy(wt_sg[:].rearrange("p (t m) -> p m t", t=PACK), wt_s[:].indirect(wt_list[:]))
-        wt_wd = sb.tile([P, R], U16, name="wt_wd", align_bytes=64)
-        nc.vector.tensor_copy(wt_wd[:].rearrange("p (t m) -> p t m", t=PACK), wt_wg[:].rearrange("p (m t) -> p t m", t=PACK))
-
-        inc = sb.tile([P, PACK, J], F32, name="inc", align_bytes=64)
-        for t in range(PACK):
-            ca_g = sb.tile([P, J], U8, name="ca_g%d" % t, align_bytes=64)
-            nc.vector.tensor_copy(ca_g[:], ca_t[t][:].indirect(ca_list[:]))
-            nc.scalar.activation(g[t][:, 1 : J + 1], ca_g[:].bitcast(E4M3), ACT.Copy, scale=step[:, t : t + 1])
-            nc.gpsimd.tensor_tensor(inc[:, t, :], g[t][:, 1 : J + 1], g[t][:, 0:J], ALU.subtract)
+        xt_sg = sb.tile([P, J], U8, name="xt_sg", align_bytes=64)
+        nc.vector.tensor_copy(xt_sg[:], xt_s[:].indirect(xt_list[:]))
 
         a_ps = []
-        for h in range(2):
-            cols = xt_list[:, h * LIST_COLS : (h + 1) * LIST_COLS]
+        for h in range(HALVES):
             xt_wg = sb.tile([P, HALF], U32, name="xt_wg%d" % h, align_bytes=64)
-            nc.vector.tensor_copy(xt_wg[:], xt_w[:].indirect(cols))
-            xt_sg = sb.tile([P, HALF], U8, name="xt_sg%d" % h, align_bytes=64)
-            nc.vector.tensor_copy(xt_sg[:], xt_s[:].indirect(cols))
+            nc.vector.tensor_copy(xt_wg[:], xt_w[:].indirect(xt_list[:, h * HALF // GROUP : (h + 1) * HALF // GROUP]))
             bank = ps.tile([P, PACK, HALF], F32, name="a_ps%d" % h)
             for t in range(PACK):
                 nc.tensor.matmul_mx(
@@ -98,29 +109,28 @@ def tile_list_increments_kernel(tc, xt_words, xt_scales, wt_words, wt_scales, ca
                     lhsT=wt_wd[:, t * P : (t + 1) * P].bitcast(E2M1X4),
                     lhsT_scale=wt_sg[:, t * P : (t + 1) * P],
                     rhs=xt_wg[:].bitcast(E5M2X4),
-                    rhs_scale=xt_sg[:],
+                    rhs_scale=xt_sg[:, h * HALF : (h + 1) * HALF],
                     start=True,
                     stop=True,
                 )
             a_ps.append(bank)
 
         hid = []
-        for h in range(2):
+        for h in range(HALVES):
             hid_h = sb.tile([P, HALF * PACK], BF16, name="hid%d" % h, align_bytes=64)
             nc.vector.tensor_tensor(
-                hid_h[:].rearrange("p (c i t) -> p c t i", i=2, t=PACK),
-                a_ps[h][:].rearrange("p t (c i) -> p c t i", i=2),
-                inc[:, :, h * HALF : (h + 1) * HALF].rearrange("p t (c i) -> p c t i", i=2),
+                hid_h[:].rearrange("p (c i t) -> p c t i", i=PAIR, t=PACK),
+                a_ps[h][:].rearrange("p t (c i) -> p c t i", i=PAIR),
+                inc[:, :, h * HALF : (h + 1) * HALF].rearrange("p t (c i) -> p c t i", i=PAIR),
                 ALU.mult,
             )
             hid.append(hid_h)
 
-        res = [sb.tile([P, J], F32, name="res%d" % b, align_bytes=64) for b in range(2)]
-        for h in range(2):
+        for h in range(HALVES):
             hid_w = sb.tile([P, HALF], U32, name="hid_w%d" % h, align_bytes=64)
             hid_s = sb.tile([P, HALF], U8, name="hid_s%d" % h, align_bytes=64)
             nc.vector.quantize_mx(out=hid_w[:].bitcast(E4M3X4), scales=hid_s[:], in_=hid[h][:])
-            for b in range(2):
+            for b in range(N // P):
                 acc = ps.tile([P, HALF], F32, name="o_ps%d%d" % (h, b))
                 nc.tensor.matmul_mx(
                     out=acc[:],
@@ -131,9 +141,10 @@ def tile_list_increments_kernel(tc, xt_words, xt_scales, wt_words, wt_scales, ca
                     start=True,
                     stop=True,
                 )
+                res = sb.tile([P, HALF], F32, name="res%d%d" % (h, b), align_bytes=64)
                 if b == 0:
-                    nc.scalar.copy(res[b][:, h * HALF : (h + 1) * HALF], acc[:])
+                    nc.scalar.copy(res[:], acc[:])
                 else:
-                    nc.vector.tensor_copy(res[b][:, h * HALF : (h + 1) * HALF], acc[:])
-        nc.scalar.dma_start(out[0:P, :], res[0][:])
-        nc.sync.dma_start(out[P : 2 * P, :], res[1][:])
+                    nc.vector.tensor_copy(res[:], acc[:])
+                queue = nc.scalar if (h, b) == (HALVES - 1, 0) else nc.sync
+                queue.dma_start(out[b * P : (b + 1) * P, h * HALF : (h + 1) * HALF], res[:])

from contextlib import ExitStack

import concourse.mybir as mybir

K, T, J, R, V, D, N = 512, 1024, 256, 512, 1024, 2048, 256
FLOPS = 2 * K * R * J + 2 * R * N * J

F32 = mybir.dt.float32
BF16 = mybir.dt.bfloat16
I32 = mybir.dt.int32
U32 = mybir.dt.uint32
U16 = mybir.dt.uint16
U8 = mybir.dt.uint8
E4M3 = mybir.dt.float8_e4m3fn
E4M3X4 = mybir.dt.float8_e4m3fn_x4
E5M2X4 = mybir.dt.float8_e5m2_x4
E2M1X4 = mybir.dt.float4_e2m1fn_x4
ALU = mybir.AluOpType
ACT = mybir.ActivationFunctionType

P = 128
PACK = 4
GROUP = 16
QUADRANT = 32
SCALE_ROWS = 4
HALVES = 2
HALF = J // HALVES
G_COLS = J + 8
PAIR = 2


def load_scale_rows(nc, plane, scales):
    for q in range(P // QUADRANT):
        rows = scales[0, SCALE_ROWS * q : SCALE_ROWS * (q + 1), :]
        nc.sync.dma_start(plane[QUADRANT * q : QUADRANT * q + SCALE_ROWS, :].bitcast(I32), rows.bitcast(I32))


def tile_list_increments_kernel(tc, xt_words, xt_scales, wt_words, wt_scales, ca, st, wb_words, wb_scales, offs, offs2, offs3, out):
    nc = tc.nc
    with ExitStack() as ctx:
        sb = ctx.enter_context(tc.tile_pool(name="sb", bufs=1))
        ps = ctx.enter_context(tc.psum_pool(name="ps", bufs=1))

        wt_list = sb.tile([P, R // GROUP], U16, name="wt_list")
        xt_list = sb.tile([P, J // GROUP], U16, name="xt_list")
        ca_list = sb.tile([P, J // GROUP], U16, name="ca_list")
        wt_w = sb.tile([P, V], U16, name="wt_w", align_bytes=64)
        wt_s = sb.tile([P, V], U8, name="wt_s", align_bytes=64)
        xt_w = sb.tile([P, T], U32, name="xt_w", align_bytes=64)
        xt_s = sb.tile([P, T], U8, name="xt_s", align_bytes=64)
        wb_w = sb.tile([P, 2 * N], U8, name="wb_w", align_bytes=64)
        wb_s = sb.tile([P, N], U8, name="wb_s", align_bytes=64)
        ca_t = [sb.tile([P, D], U8, name="ca_t%d" % t, tag="ca_t%d" % t, align_bytes=64) for t in range(PACK)]
        step = sb.tile([P, PACK], F32, name="step")
        g = sb.tile([P, PACK, G_COLS], F32, name="g", align_bytes=64)
        zero = sb.tile([P, PACK], F32, name="zero")

        nc.vector.memset(wt_s[:].bitcast(I32), 0)
        nc.vector.memset(xt_s[:].bitcast(I32), 0)
        nc.vector.memset(wb_s[:].bitcast(I32), 0)
        nc.vector.memset(zero[:], 0.0)

        ca_rows = ca.rearrange("(p t) d -> p t d", t=PACK)
        nc.sync.dma_start(wt_list[:], offs)
        nc.scalar.dma_start(wt_w[:].bitcast(I32), wt_words[0].bitcast(I32))
        nc.sync.dma_start(ca_list[:], offs3)
        nc.sync.dma_start(ca_t[0][:], ca_rows[:, 0, :])
        nc.scalar.dma_start(step[:], st.rearrange("(p t) o -> p (t o)", t=PACK))
        for t in range(1, PACK):
            nc.sync.dma_start(ca_t[t][:], ca_rows[:, t, :])
        load_scale_rows(nc, wt_s, wt_scales)
        nc.sync.dma_start(xt_list[:], offs2)
        load_scale_rows(nc, xt_s, xt_scales)
        nc.sync.dma_start(xt_w[:].bitcast(I32), xt_words[0].rearrange("p c r -> p (c r)").bitcast(I32))
        nc.sync.dma_start(wb_w[:].bitcast(I32), wb_words[0].bitcast(I32))
        load_scale_rows(nc, wb_s, wb_scales)

        nc.scalar.activation(g[:, :, 0], zero[:], ACT.Copy)

        inc = sb.tile([P, PACK, J], F32, name="inc", align_bytes=64)

        def increments(t):
            ca_g = sb.tile([P, J], U8, name="ca_g%d" % t, align_bytes=64)
            nc.vector.tensor_copy(ca_g[:], ca_t[t][:].indirect(ca_list[:]))
            nc.scalar.activation(g[:, t, 1 : J + 1], ca_g[:].bitcast(E4M3), ACT.Copy, scale=step[:, t : t + 1])
            nc.gpsimd.tensor_tensor(inc[:, t, :], g[:, t, 1 : J + 1], g[:, t, 0:J], ALU.subtract)

        wt_wg = sb.tile([P, R], U16, name="wt_wg", align_bytes=64)
        nc.vector.tensor_copy(wt_wg[:], wt_w[:].indirect(wt_list[:]))
        increments(0)
        wt_wd = sb.tile([P, R], U16, name="wt_wd", tag="ca_t0", align_bytes=64)
        nc.vector.tensor_copy(wt_wd[:].rearrange("p (t m) -> p t m", t=PACK), wt_wg[:].rearrange("p (m t) -> p t m", t=PACK))
        for t in range(1, PACK):
            increments(t)

        wt_sg = sb.tile([P, R], U8, name="wt_sg", align_bytes=64)
        nc.vector.tensor_copy(wt_sg[:].rearrange("p (t m) -> p m t", t=PACK), wt_s[:].indirect(wt_list[:]))
        xt_sg = sb.tile([P, J], U8, name="xt_sg", align_bytes=64)
        nc.vector.tensor_copy(xt_sg[:], xt_s[:].indirect(xt_list[:]))

        a_ps = []
        for h in range(HALVES):
            xt_wg = sb.tile([P, HALF], U32, name="xt_wg%d" % h, align_bytes=64)
            nc.vector.tensor_copy(xt_wg[:], xt_w[:].indirect(xt_list[:, h * HALF // GROUP : (h + 1) * HALF // GROUP]))
            bank = ps.tile([P, PACK, HALF], F32, name="a_ps%d" % h)
            for t in range(PACK):
                nc.tensor.matmul_mx(
                    out=bank[:, t, :],
                    lhsT=wt_wd[:, t * P : (t + 1) * P].bitcast(E2M1X4),
                    lhsT_scale=wt_sg[:, t * P : (t + 1) * P],
                    rhs=xt_wg[:].bitcast(E5M2X4),
                    rhs_scale=xt_sg[:, h * HALF : (h + 1) * HALF],
                    start=True,
                    stop=True,
                )
            a_ps.append(bank)

        hid = []
        for h in range(HALVES):
            hid_h = sb.tile([P, HALF * PACK], BF16, name="hid%d" % h, align_bytes=64)
            nc.vector.tensor_tensor(
                hid_h[:].rearrange("p (c i t) -> p c t i", i=PAIR, t=PACK),
                a_ps[h][:].rearrange("p t (c i) -> p c t i", i=PAIR),
                inc[:, :, h * HALF : (h + 1) * HALF].rearrange("p t (c i) -> p c t i", i=PAIR),
                ALU.mult,
            )
            hid.append(hid_h)

        for h in range(HALVES):
            hid_w = sb.tile([P, HALF], U32, name="hid_w%d" % h, align_bytes=64)
            hid_s = sb.tile([P, HALF], U8, name="hid_s%d" % h, align_bytes=64)
            nc.vector.quantize_mx(out=hid_w[:].bitcast(E4M3X4), scales=hid_s[:], in_=hid[h][:])
            for b in range(N // P):
                acc = ps.tile([P, HALF], F32, name="o_ps%d%d" % (h, b))
                nc.tensor.matmul_mx(
                    out=acc[:],
                    lhsT=wb_w[:, 2 * b * P : 2 * (b + 1) * P].bitcast(E2M1X4),
                    lhsT_scale=wb_s[:, b * P : (b + 1) * P],
                    rhs=hid_w[:].bitcast(E4M3X4),
                    rhs_scale=hid_s[:],
                    start=True,
                    stop=True,
                )
                res = sb.tile([P, HALF], F32, name="res%d%d" % (h, b), align_bytes=64)
                if b == 0:
                    nc.scalar.copy(res[:], acc[:])
                else:
                    nc.vector.tensor_copy(res[:], acc[:])
                queue = nc.scalar if (h, b) == (HALVES - 1, 0) else nc.sync
                queue.dma_start(out[b * P : (b + 1) * P, h * HALF : (h + 1) * HALF], res[:])
